import numpy as np
import ml_dtypes


def mxq(x, axis, fmt="e4m3"):
    dtype, down = {"e4m3": (ml_dtypes.float8_e4m3fn, 7), "e5m2": (ml_dtypes.float8_e5m2, 14)}[fmt]
    v = np.moveaxis(np.asarray(x, np.float32).astype(ml_dtypes.bfloat16).astype(np.float64), axis, -1)
    blocks = v.reshape(v.shape[:-1] + (-1, 32))
    amax = np.abs(blocks).max(-1, keepdims=True)
    byte = np.maximum(np.where(amax > 0, np.frexp(amax)[1] - 1 + 127, 0) - down, 1)
    scale = np.exp2(byte - 127.0)
    codes = (blocks / scale).astype(np.float32).astype(dtype).astype(np.float64)
    return np.moveaxis((codes * scale).reshape(v.shape), -1, axis)


WIDE = False


def mx_kscale(k):
    if not WIDE:
        return np.ones(k)
    levels = np.array([10, -10, 5, -5, 0])
    if k % 512:
        return np.exp2(np.random.permutation(np.resize(levels, k // 32))).repeat(32)
    a = np.empty((k // 512, 16))
    for p in range(k // 512):
        a[p, :8] = np.random.permutation(np.resize(levels, 8))
        for g in range(8):
            far = levels[np.abs(levels - a[p, g]) >= 10]
            a[p, g + 8] = far[np.random.randint(len(far))]
    return np.exp2(a.ravel()).repeat(32)


BF16 = ml_dtypes.bfloat16


def bf(x):
    return np.asarray(x, np.float32).astype(BF16)


def f64(x):
    return np.asarray(x).astype(np.float64)


E2M1 = np.array([0.0, 0.5, 1.0, 1.5, 2.0, 3.0, 4.0, 6.0, -0.0, -0.5, -1.0, -1.5, -2.0, -3.0, -4.0, -6.0])


def pack_weight(w, fmt):
    k, n = w.shape
    w = f64(bf(w)).reshape(k // 32, 32, n)
    amax = np.abs(w).max(1)
    if fmt == "e4m3":
        byte = np.frexp(amax)[1] - 1 + 127 - 7
    else:
        mant, ex = np.frexp(amax / 6.0)
        byte = np.where(mant > 0.5, ex, ex - 1) + 127
    byte = np.clip(np.where(amax > 0, byte, 1), 1, 254)
    scaled = (w * np.exp2(127.0 - byte)[:, None, :]).reshape(k, n).astype(np.float32)
    by_word = np.ascontiguousarray(scaled.reshape(k // 512, 128, 4, n).transpose(0, 1, 3, 2))
    if fmt == "e4m3":
        words = by_word.astype(ml_dtypes.float8_e4m3fn).view(np.uint8)
    else:
        c = by_word.astype(ml_dtypes.float4_e2m1fn).view(np.uint8) & 0xF
        words = c[..., 0::2] | (c[..., 1::2] << 4)
    return np.ascontiguousarray(words), np.ascontiguousarray(byte.astype(np.uint8).reshape(k // 512, 16, n))


def unpack_weight(words, scales, fmt):
    g, p, n, _ = words.shape
    if fmt == "e4m3":
        vals = np.ascontiguousarray(words).view(ml_dtypes.float8_e4m3fn).astype(np.float64)
    else:
        nib = np.empty((g, p, n, 4), np.uint8)
        nib[..., 0::2] = words & 0xF
        nib[..., 1::2] = words >> 4
        vals = E2M1[nib]
    vals = vals * np.repeat(np.exp2(scales.astype(np.float64) - 127.0), 8, axis=1)[..., None]
    return vals.transpose(0, 1, 3, 2).reshape(g * 512, n)

E4M3FN = np.array([(-1.0 if i & 128 else 1.0) * ((1.0 + (i & 7) / 8.0) * 2.0 ** (((i >> 3) & 15) - 7) if i & 120 else (i & 7) * 2.0 ** -9) for i in range(256)])


def e4m3fn_bytes(y):
    return np.clip(np.asarray(y, np.float64), -448.0, 448.0).astype(np.float32).astype(ml_dtypes.float8_e4m3fn).view(np.uint8)


def e4m3fn_values(b):
    return E4M3FN[b]


B, Z, F, U, T = 1024, 512, 1024, 128, 3


def draw0():
    s, t = mx_kscale(Z), mx_kscale(F)
    zbar = np.random.standard_normal((B, Z)) * s
    mean = np.random.standard_normal((B, Z))
    var = np.random.uniform(0.5, 2.0, (B, 1)) * np.random.uniform(0.5, 1.5, (B, Z))
    u = np.random.standard_normal((B, U))
    w1 = np.random.standard_normal((Z, F)) / np.sqrt(Z) / s[:, None] * t[None, :]
    w2 = np.random.standard_normal((T, F, Z)) * 1.4 / np.sqrt(F) / t[None, :, None]
    bmat = np.random.standard_normal((U, Z)) / np.sqrt(U)
    w1_words, w1_scales = pack_weight(w1, "e4m3")
    return {"zbar": bf(zbar), "mean": bf(mean), "var": bf(var), "u": bf(u), "w1_words": w1_words, "w1_scales": w1_scales, "w2": bf(w2), "bmat": bf(bmat)}


def transition_params(zbar, w1, w2):
    h = np.maximum(mxq(zbar, 1, "e4m3") @ w1, 0.0)
    hq = mxq(h, 1, "e4m3")
    v = hq @ mxq(w2[0], 0, "e4m3")
    r = hq @ mxq(w2[1], 0, "e4m3")
    o = hq @ mxq(w2[2], 0, "e4m3")
    return v, r, o


def core(zbar, mean, var, u, w1_words, w1_scales, w2, bmat):
    zbar, mean, var, u = f64(zbar), f64(mean), f64(var), f64(u)
    w1, w2, bmat = unpack_weight(w1_words, w1_scales, "e4m3"), f64(w2), f64(bmat)
    inv_sqrt_z = 1.0 / np.sqrt(Z)
    inv_z = 1.0 / Z

    v, r, o = transition_params(zbar, w1, w2)

    d = inv_sqrt_z * np.sum(r * mean, axis=1)
    mean_next = mean + v * d[:, None] + o + u @ bmat

    s = inv_z * np.sum(np.square(r) * var, axis=1)
    var_next = var + (2.0 * inv_sqrt_z) * v * r * var + np.square(v) * s[:, None]

    return mean_next, var_next


def setup_inputs():
    drawn = draw0()
    full = np.asarray(drawn['w2']).astype(np.float64)
    scale = (np.abs(full).reshape(3, 8, 128, 4, 128).max(axis=(2, 4)) / 448.0).astype(np.float32)
    given = {}
    for key, value in drawn.items():
        if key == 'w2':
            given['w2_bytes'] = e4m3fn_bytes(full / np.repeat(np.repeat(scale.astype(np.float64), 128, axis=1), 128, axis=2))
            given['w2_scale'] = scale
        else:
            given[key] = value
    return given


def reference(zbar, mean, var, u, w1_words, w1_scales, w2_bytes, w2_scale, bmat):
    return core(zbar, mean, var, u, w1_words, w1_scales, e4m3fn_values(w2_bytes) * np.repeat(np.repeat(w2_scale.astype(np.float64), 128, axis=1), 128, axis=2), bmat)

@@ -1,0 +1,301 @@
+from contextlib import ExitStack
+
+import concourse.mybir as mybir
+from concourse.masks import make_identity
+
+B, Z, F, U, T = 1024, 512, 1024, 128, 3
+P = 128
+NT = B // P
+FLOPS = 2 * B * Z * F + 2 * T * B * F * Z + 2 * B * U * Z
+
+F32 = mybir.dt.float32
+BF16 = mybir.dt.bfloat16
+U32 = mybir.dt.uint32
+I32 = mybir.dt.int32
+U8 = mybir.dt.uint8
+F8 = mybir.dt.float8_e4m3fn
+X4 = mybir.dt.float8_e4m3fn_x4
+ADD = mybir.AluOpType.add
+MULT = mybir.AluOpType.mult
+ACT = mybir.ActivationFunctionType
+
+INV = 1.0 / Z ** 0.5
+CROSS = 2.0 * INV
+
+
+def tile_e2crankonelocallylinearbeliefstep_d2p_kernel(tc, zbar, mean, var, u, w1_words, w1_scales, w2_bytes, w2_scale, bmat, out_0, out_1):
+    nc = tc.nc
+    with ExitStack() as ctx:
+        keep = ctx.enter_context(tc.tile_pool(name="keep", bufs=1))
+        work = ctx.enter_context(tc.tile_pool(name="work", bufs=3))
+        psum = ctx.enter_context(tc.psum_pool(name="psum", bufs=1))
+
+        def kt(name, shape, dtype):
+            return keep.tile(shape, dtype, name=name, align_bytes=64)
+
+        ident_f = kt("ident_f", [P, P], F32)
+        ident_b = kt("ident_b", [P, P], BF16)
+        zb = kt("zb", [P, NT, Z], BF16)
+        w1_raw = kt("w1_raw", [P, F], U32)
+        w1_sraw = kt("w1_sraw", [P, F], U8)
+        w1_c = kt("w1_c", [P, F], U32)
+        w1_s = kt("w1_s", [P, F], U8)
+        sc_all = kt("sc_all", [P, 96], F32)
+        sc = kt("sc", [P, 24], F32)
+        by = {}
+        wd = {}
+        wi = {}
+        w2c = {}
+        w2s = {}
+        for a in range(3):
+            for g in range(2):
+                by[a, g] = kt("by%d%d" % (a, g), [P, 4 * Z], U8)
+                wd[a, g] = kt("wd%d%d" % (a, g), [P, 4, Z], BF16)
+                wi[a, g] = kt("wi%d%d" % (a, g), [P, Z, 4], BF16)
+                w2c[a, g] = kt("w2c%d%d" % (a, g), [P, Z], U32)
+                w2s[a, g] = kt("w2s%d%d" % (a, g), [P, Z], U8)
+        mean_t = kt("mean_t", [P, NT, Z], BF16)
+        var_t = kt("var_t", [P, NT, Z], BF16)
+        u_t = kt("u_t", [P, NT, U], BF16)
+        ut = kt("ut", [P, NT, P], BF16)
+        bm = kt("bm", [P, Z], BF16)
+        base = kt("base", [P, NT, Z], F32)
+        rvt = kt("rvt", [P, NT, Z], F32)
+        junk = kt("junk", [P, Z], F32)
+        d_col = [kt("d%d" % b, [P, 1], F32) for b in range(NT)]
+        s_col = [kt("s%d" % b, [P, 1], F32) for b in range(NT)]
+
+        zbar_v = zbar.rearrange("(p b) k -> p b k", b=NT)
+        mean_v = mean.rearrange("(p b) k -> p b k", b=NT)
+        var_v = var.rearrange("(p b) k -> p b k", b=NT)
+        u_v = u.rearrange("(p b) k -> p b k", b=NT)
+        out0_v = out_0.rearrange("(p b) n -> p b n", b=NT)
+        out1_v = out_1.rearrange("(p b) n -> p b n", b=NT)
+        w2_v = w2_bytes.rearrange("a (g p t) n -> a g p (t n)", g=2, t=4)
+
+        WM = {"10":["v","gggg"],"11":["v","ggvv"],"20":["s","gggg"],"21":["s","ssss"],"00":["s","vvvv"],"01":["s","gggg"]}
+        AG = [4,5,6,7]
+        DG = [3,4,5,6]
+        DV = [7]
+        EG = []
+        XB, AB, OB = 2, 4, 2
+        nc.vector.memset(w1_sraw[:].bitcast(I32), 0)
+        nc.gpsimd.dma_start(out=sc_all[:], in_=w2_scale.rearrange("a i j -> (a i j)").partition_broadcast(P))
+        nc.sync.dma_start(out=by[1, 0][:], in_=w2_v[1, 0])
+        for q in range(4):
+            nc.sync.dma_start(out=w1_sraw[32 * q:32 * q + 4, :].bitcast(I32), in_=w1_scales[0, 4 * q:4 * q + 4, :].bitcast(I32))
+        nc.sync.dma_start(out=zb[:, 0:2, :], in_=zbar_v[:, 0:2, :])
+        nc.sync.dma_start(out=w1_raw[:].bitcast(I32), in_=w1_words[0].rearrange("p n t -> p (n t)").bitcast(I32))
+        nc.sync.dma_start(out=by[1, 1][:], in_=w2_v[1, 1])
+        nc.sync.dma_start(out=by[0, 0][:], in_=w2_v[0, 0])
+        nc.sync.dma_start(out=zb[:, 2:4, :], in_=zbar_v[:, 2:4, :])
+        nc.sync.dma_start(out=by[0, 1][:], in_=w2_v[0, 1])
+        nc.sync.dma_start(out=zb[:, 4:6, :], in_=zbar_v[:, 4:6, :])
+        nc.sync.dma_start(out=zb[:, 6:8, :], in_=zbar_v[:, 6:8, :])
+        nc.sync.dma_start(out=var_t[:, 0:4, :], in_=var_v[:, 0:4, :])
+        nc.sync.dma_start(out=mean_t[:, 0:4, :], in_=mean_v[:, 0:4, :])
+        nc.sync.dma_start(out=u_t[:], in_=u_v)
+        nc.sync.dma_start(out=bm[:], in_=bmat)
+        nc.sync.dma_start(out=by[2, 0][:], in_=w2_v[2, 0])
+        nc.sync.dma_start(out=by[2, 1][:], in_=w2_v[2, 1])
+        nc.sync.dma_start(out=var_t[:, 4:8, :], in_=var_v[:, 4:8, :])
+        nc.sync.dma_start(out=mean_t[:, 4:8, :], in_=mean_v[:, 4:8, :])
+
+        make_identity(nc, ident_f[:])
+        sc_view = sc_all[:].rearrange("p (a g q j) -> p q a g j", a=3, g=2, q=4, j=4)
+        sc_out = sc[:].rearrange("p (a g j) -> p a g j", a=3, g=2, j=4)
+        for q in range(4):
+            nc.gpsimd.tensor_copy(out=sc_out[32 * q:32 * q + 32], in_=sc_view[32 * q:32 * q + 32, q])
+        make_identity(nc, ident_b[:])
+        nc.vector.tensor_copy(out=w1_s[:].rearrange("p (g t m) -> p g t m", g=2, t=4), in_=w1_sraw[:].rearrange("p (g m t) -> p g t m", g=2, t=4))
+        nc.vector.tensor_copy(out=w1_c[:].bitcast(I32).rearrange("p (g t m) -> p g t m", g=2, t=4), in_=w1_raw[:].bitcast(I32).rearrange("p (g m t) -> p g t m", g=2, t=4))
+
+        zwords = zb[:].rearrange("p b k -> p (b k)").bitcast(F32)
+        zq = {}
+        hq = {}
+        t3 = {}
+
+        def quant(x, width, name):
+            cc = keep.tile([P, width], U32, name=name + "c", align_bytes=64)
+            ss = keep.tile([P, width], U8, name=name + "s", align_bytes=64)
+            nc.vector.quantize_mx(out=cc[:].bitcast(X4), scales=ss[:], in_=x)
+            return cc, ss
+
+        def pair(i):
+            bank = psum.tile([P, 2, 2, P], F32, name="xz%d" % i, tag="x", bufs=XB)
+            for bb in range(2):
+                o = (2 * i + bb) * 256
+                for h in range(2):
+                    nc.tensor.transpose(bank[:, bb, h, :], zwords[:, o + h:o + 256:2], ident_f[:])
+            zg = work.tile([P, 2, P, 4], BF16, name="zg%d" % i, tag="zg", bufs=3, align_bytes=64)
+            nc.scalar.copy(out=zg[:].rearrange("p b r k -> p (b r k)").bitcast(F32).rearrange("p (b r h) -> p b r h", b=2, h=2), in_=bank[:].rearrange("p b h r -> p b r h"))
+            zq[i] = quant(zg[:].rearrange("p b r k -> p (b r k)"), 2 * P, "zq%d" % i)
+
+        def hidden(b):
+            i, bb = b // 2, b % 2
+            cc, ss = zq[i]
+            hb = work.tile([P, 2, P, 4], BF16, name="hb%d" % b, tag="hb", bufs=3, align_bytes=64)
+            for g in range(2):
+                bank = psum.tile([P, 4, P], F32, name="xs%d_%d" % (b, g), tag="x", bufs=XB)
+                for t in range(4):
+                    o = (4 * g + t) * P
+                    nc.tensor.matmul_mx(out=bank[:, t, :], lhsT=w1_c[:, o:o + P].bitcast(X4), lhsT_scale=w1_s[:, o:o + P],
+                                        rhs=cc[:, bb * P:bb * P + P].bitcast(X4), rhs_scale=ss[:, bb * P:bb * P + P], start=True, stop=True)
+                nc.scalar.activation(out=hb[:, g], in_=bank[:].rearrange("p t m -> p m t"), func=ACT.Relu)
+            hq[b] = quant(hb[:].rearrange("p g m t -> p (g m t)"), 2 * P, "hq%d" % b)
+
+        def weights(a, g):
+            wide, inter = WM["%d%d" % (a, g)]
+            src = by[a, g][:].bitcast(F8)
+            dst = wd[a, g][:].rearrange("p t n -> p (t n)")
+            col = (a * 2 + g) * 4
+            if wide == "s":
+                nc.scalar.copy(out=dst, in_=src)
+            elif wide == "v":
+                nc.vector.tensor_copy(out=dst, in_=src)
+            else:
+                for k in range(16):
+                    sl = slice(k * P, k * P + P)
+                    cs = sc[:, col + k % 4:col + k % 4 + 1]
+                    if wide == "S":
+                        nc.scalar.activation(out=dst[:, sl], in_=src[:, sl], func=ACT.Copy, scale=cs)
+                    else:
+                        nc.vector.tensor_scalar(dst[:, sl], src[:, sl], cs, None, MULT)
+            if inter in ("G", "V", "S"):
+                src = wd[a, g][:].rearrange("p t n -> p n t")
+                dst = wi[a, g][:]
+                if inter == "G":
+                    nc.gpsimd.tensor_scalar(dst, src, 1.0, 0.0, MULT, ADD)
+                elif inter == "V":
+                    nc.vector.tensor_copy(out=dst, in_=src)
+                else:
+                    nc.scalar.copy(out=dst, in_=src)
+            else:
+                for j in range(4):
+                    src = wd[a, g][:, :, P * j:P * j + P].rearrange("p t n -> p n t")
+                    dst = wi[a, g][:, P * j:P * j + P, :]
+                    cs = sc[:, col + j:col + j + 1]
+                    if inter[j] == "g":
+                        nc.gpsimd.tensor_scalar(dst, src, cs, 0.0, MULT, ADD)
+                    elif inter[j] == "s":
+                        nc.scalar.activation(out=dst, in_=src, func=ACT.Copy, scale=cs)
+                    else:
+                        nc.vector.tensor_scalar(dst, src, cs, None, MULT)
+            nc.vector.quantize_mx(out=w2c[a, g][:].bitcast(X4), scales=w2s[a, g][:], in_=wi[a, g][:].rearrange("p n t -> p (n t)"))
+
+        def product(a, b, tag, bufs):
+            bank = psum.tile([P, Z], F32, name="ps%d_%d" % (a, b), tag=tag, bufs=bufs)
+            cc, ss = hq[b]
+            for g in range(2):
+                nc.tensor.matmul_mx(out=bank[:], lhsT=cc[:, g * P:g * P + P].bitcast(X4), lhsT_scale=ss[:, g * P:g * P + P],
+                                    rhs=w2c[a, g][:].bitcast(X4), rhs_scale=w2s[a, g][:], start=(g == 0), stop=(g == 1))
+            return bank
+
+        def u_step():
+            for k in range(2):
+                bank = psum.tile([P, 4, P], BF16, name="xu%d" % k, tag="x", bufs=XB)
+                for b in range(4):
+                    nc.tensor.transpose(bank[:, b, :], u_t[:, 4 * k + b, :], ident_b[:])
+                nc.scalar.copy(out=ut[:, 4 * k:4 * k + 4, :], in_=bank[:])
+
+        def base_step(b):
+            bank = psum.tile([P, Z], F32, name="xb%d" % b, tag="x", bufs=XB)
+            nc.tensor.matmul(bank[:], lhsT=ut[:, b, :], rhs=bm[:], start=True, stop=False)
+            nc.tensor.matmul(bank[:], lhsT=ident_b[:], rhs=mean_t[:, b, :], start=False, stop=True)
+            nc.scalar.copy(out=base[:, b, :], in_=bank[:])
+
+        def r_step(b):
+            r = product(1, b, "a", AB)
+            if b in AG:
+                rs = work.tile([P, Z], F32, name="rs%d" % b, tag="rs", bufs=2)
+                nc.scalar.activation(out=rs[:], in_=r[:], func=ACT.Copy, scale=CROSS)
+                nc.gpsimd.tensor_tensor(rvt[:, b, :], rs[:], var_t[:, b, :], op=MULT)
+            else:
+                nc.vector.scalar_tensor_tensor(rvt[:, b, :], r[:], CROSS, var_t[:, b, :], MULT, MULT)
+            jd = work.tile([P, Z], F32, name="jd%d" % b, tag="jd", bufs=1)
+            nc.vector.scalar_tensor_tensor(jd[:], r[:], INV, mean_t[:, b, :], MULT, MULT, accum_out=d_col[b][:])
+            js = work.tile([P, Z], F32, name="js%d" % b, tag="js", bufs=1)
+            nc.vector.scalar_tensor_tensor(js[:], r[:], 1.0 / (Z * CROSS), rvt[:, b, :], MULT, MULT, accum_out=s_col[b][:])
+
+        def v_step(b):
+            v = product(0, b, "a", AB)
+            sv = work.tile([P, Z], F32, name="sv%d" % b, tag="sv", bufs=3)
+            if b in DG:
+                tmp = work.tile([P, Z], F32, name="st%d" % b, tag="st", bufs=2)
+                nc.scalar.activation(out=tmp[:], in_=v[:], func=ACT.Copy, scale=s_col[b][:])
+                nc.gpsimd.tensor_tensor(sv[:], tmp[:], rvt[:, b, :], op=ADD)
+            else:
+                nc.vector.scalar_tensor_tensor(sv[:], v[:], s_col[b][:], rvt[:, b, :], MULT, ADD)
+            t3[b] = work.tile([P, Z], F32, name="t3_%d" % b, tag="t3", bufs=4)
+            nc.vector.scalar_tensor_tensor(t3[b][:], v[:], d_col[b][:], base[:, b, :], MULT, ADD)
+            t2 = work.tile([P, Z], F32, name="t2_%d" % b, tag="t2", bufs=3)
+            nc.vector.tensor_tensor(t2[:], v[:], sv[:], op=MULT)
+            vo = work.tile([P, Z], F32, name="vo_%d" % b, tag="vo", bufs=5)
+            if b in DV:
+                nc.vector.tensor_tensor(vo[:], t2[:], var_t[:, b, :], op=ADD)
+            else:
+                nc.gpsimd.tensor_tensor(vo[:], t2[:], var_t[:, b, :], op=ADD)
+            nc.sync.dma_start(out=out1_v[:, b, :], in_=vo[:])
+
+        def o_step(b):
+            o = product(2, b, "o", OB)
+            mo = work.tile([P, Z], F32, name="mo_%d" % b, tag="mo", bufs=5)
+            if b in EG:
+                oc = work.tile([P, Z], F32, name="os%d" % b, tag="os", bufs=2)
+                nc.scalar.copy(out=oc[:], in_=o[:])
+                nc.gpsimd.tensor_tensor(mo[:], oc[:], t3[b][:], op=ADD)
+            else:
+                nc.vector.tensor_tensor(mo[:], o[:], t3[b][:], op=ADD)
+            nc.sync.dma_start(out=out0_v[:, b, :], in_=mo[:])
+
+        weights(1, 0)
+        pair(0)
+        weights(1, 1)
+        hidden(0)
+        pair(1)
+        hidden(1)
+        weights(0, 0)
+        r_step(0)
+        pair(2)
+        hidden(2)
+        weights(0, 1)
+        r_step(1)
+        pair(3)
+        hidden(3)
+        weights(2, 0)
+        u_step()
+        r_step(2)
+        base_step(0)
+        weights(2, 1)
+        r_step(3)
+        base_step(1)
+        v_step(0)
+        hidden(4)
+        r_step(4)
+        base_step(2)
+        v_step(1)
+        o_step(0)
+        hidden(5)
+        r_step(5)
+        base_step(3)
+        v_step(2)
+        o_step(1)
+        hidden(6)
+        r_step(6)
+        base_step(4)
+        v_step(3)
+        o_step(2)
+        hidden(7)
+        r_step(7)
+        base_step(5)
+        v_step(4)
+        o_step(3)
+        base_step(6)
+        v_step(5)
+        o_step(4)
+        base_step(7)
+        v_step(6)
+        o_step(5)
+        v_step(7)
+        o_step(6)
+        o_step(7)

@@ -29,6 +29,7 @@ def tile_e2crankonelocallylinearbeliefstep_d2p_kernel(tc, zbar, mean, var, u, w1
         keep = ctx.enter_context(tc.tile_pool(name="keep", bufs=1))
         work = ctx.enter_context(tc.tile_pool(name="work", bufs=3))
         psum = ctx.enter_context(tc.psum_pool(name="psum", bufs=1))
+        ctx.enter_context(tc.manual_schedule())
 
         def kt(name, shape, dtype):
             return keep.tile(shape, dtype, name=name, align_bytes=64)
@@ -73,12 +74,11 @@ def tile_e2crankonelocallylinearbeliefstep_d2p_kernel(tc, zbar, mean, var, u, w1
         out1_v = out_1.rearrange("(p b) n -> p b n", b=NT)
         w2_v = w2_bytes.rearrange("a (g p t) n -> a g p (t n)", g=2, t=4)
 
-        WM = {"10":["v","gggg"],"11":["v","ggvv"],"20":["s","gggg"],"21":["s","ssss"],"00":["s","vvvv"],"01":["s","gggg"]}
-        AG = [4,5,6,7]
-        DG = [3,4,5,6]
-        DV = [7]
-        EG = []
-        XB, AB, OB = 2, 4, 2
+        WM = {"10": ["h", "ssvs"], "11": ["v", "svsv"], "20": ["v", "svvv"], "21": ["h", "svvv"], "00": ["h", "vvsv"], "01": ["h", "vssv"]}
+        DV = [6]
+        AG = []
+        EP = [0, 1, 2, 3, 4, 5, 6, 7]
+        XB, AB, OB, QB = 2, 3, 2, 1
         nc.vector.memset(w1_sraw[:].bitcast(I32), 0)
         nc.gpsimd.dma_start(out=sc_all[:], in_=w2_scale.rearrange("a i j -> (a i j)").partition_broadcast(P))
         nc.sync.dma_start(out=by[1, 0][:], in_=w2_v[1, 0])
@@ -87,17 +87,17 @@ def tile_e2crankonelocallylinearbeliefstep_d2p_kernel(tc, zbar, mean, var, u, w1
         nc.sync.dma_start(out=zb[:, 0:2, :], in_=zbar_v[:, 0:2, :])
         nc.sync.dma_start(out=w1_raw[:].bitcast(I32), in_=w1_words[0].rearrange("p n t -> p (n t)").bitcast(I32))
         nc.sync.dma_start(out=by[1, 1][:], in_=w2_v[1, 1])
-        nc.sync.dma_start(out=by[0, 0][:], in_=w2_v[0, 0])
         nc.sync.dma_start(out=zb[:, 2:4, :], in_=zbar_v[:, 2:4, :])
-        nc.sync.dma_start(out=by[0, 1][:], in_=w2_v[0, 1])
+        nc.sync.dma_start(out=by[2, 0][:], in_=w2_v[2, 0])
+        nc.sync.dma_start(out=by[2, 1][:], in_=w2_v[2, 1])
         nc.sync.dma_start(out=zb[:, 4:6, :], in_=zbar_v[:, 4:6, :])
         nc.sync.dma_start(out=zb[:, 6:8, :], in_=zbar_v[:, 6:8, :])
         nc.sync.dma_start(out=var_t[:, 0:4, :], in_=var_v[:, 0:4, :])
         nc.sync.dma_start(out=mean_t[:, 0:4, :], in_=mean_v[:, 0:4, :])
         nc.sync.dma_start(out=u_t[:], in_=u_v)
         nc.sync.dma_start(out=bm[:], in_=bmat)
-        nc.sync.dma_start(out=by[2, 0][:], in_=w2_v[2, 0])
-        nc.sync.dma_start(out=by[2, 1][:], in_=w2_v[2, 1])
+        nc.sync.dma_start(out=by[0, 0][:], in_=w2_v[0, 0])
+        nc.sync.dma_start(out=by[0, 1][:], in_=w2_v[0, 1])
         nc.sync.dma_start(out=var_t[:, 4:8, :], in_=var_v[:, 4:8, :])
         nc.sync.dma_start(out=mean_t[:, 4:8, :], in_=mean_v[:, 4:8, :])
 
@@ -105,10 +105,16 @@ def tile_e2crankonelocallylinearbeliefstep_d2p_kernel(tc, zbar, mean, var, u, w1
         sc_view = sc_all[:].rearrange("p (a g q j) -> p q a g j", a=3, g=2, q=4, j=4)
         sc_out = sc[:].rearrange("p (a g j) -> p a g j", a=3, g=2, j=4)
         for q in range(4):
-            nc.gpsimd.tensor_copy(out=sc_out[32 * q:32 * q + 32], in_=sc_view[32 * q:32 * q + 32, q])
-        make_identity(nc, ident_b[:])
-        nc.vector.tensor_copy(out=w1_s[:].rearrange("p (g t m) -> p g t m", g=2, t=4), in_=w1_sraw[:].rearrange("p (g m t) -> p g t m", g=2, t=4))
-        nc.vector.tensor_copy(out=w1_c[:].bitcast(I32).rearrange("p (g t m) -> p g t m", g=2, t=4), in_=w1_raw[:].bitcast(I32).rearrange("p (g m t) -> p g t m", g=2, t=4))
+            nc.scalar.copy(out=sc_out[32 * q:32 * q + 32], in_=sc_view[32 * q:32 * q + 32, q])
+        nc.scalar.copy(out=ident_b[:], in_=ident_f[:])
+        def Pm(k):
+            if k == 0:
+                nc.vector.tensor_copy(out=w1_s[:].rearrange("p (g t m) -> p g t m", g=2, t=4), in_=w1_sraw[:].rearrange("p (g m t) -> p g t m", g=2, t=4))
+            else:
+                g = k - 1
+                nc.vector.tensor_copy(out=w1_c[:, 512 * g:512 * g + 512].bitcast(I32).rearrange("p (t m) -> p t m", t=4), in_=w1_raw[:, 512 * g:512 * g + 512].bitcast(I32).rearrange("p (m t) -> p t m", t=4))
+
+        banks = {}
 
         zwords = zb[:].rearrange("p b k -> p (b k)").bitcast(F32)
         zq = {}
@@ -121,66 +127,71 @@ def tile_e2crankonelocallylinearbeliefstep_d2p_kernel(tc, zbar, mean, var, u, w1
             nc.vector.quantize_mx(out=cc[:].bitcast(X4), scales=ss[:], in_=x)
             return cc, ss
 
-        def pair(i):
-            bank = psum.tile([P, 2, 2, P], F32, name="xz%d" % i, tag="x", bufs=XB)
+        zg = {}
+        hb = {}
+        prods = {}
+        osb = {}
+        sv = {}
+        tv = {}
+
+        def Zp(i):
+            bank = banks["z", i] = psum.tile([P, 2, 2, P], F32, name="xz%d" % i, tag="x%d" % (i % 2))
             for bb in range(2):
                 o = (2 * i + bb) * 256
                 for h in range(2):
                     nc.tensor.transpose(bank[:, bb, h, :], zwords[:, o + h:o + 256:2], ident_f[:])
-            zg = work.tile([P, 2, P, 4], BF16, name="zg%d" % i, tag="zg", bufs=3, align_bytes=64)
-            nc.scalar.copy(out=zg[:].rearrange("p b r k -> p (b r k)").bitcast(F32).rearrange("p (b r h) -> p b r h", b=2, h=2), in_=bank[:].rearrange("p b h r -> p b r h"))
-            zq[i] = quant(zg[:].rearrange("p b r k -> p (b r k)"), 2 * P, "zq%d" % i)
 
-        def hidden(b):
+        def Zc(i):
+            bank = banks["z", i]
+            zg[i] = work.tile([P, 2, P, 4], BF16, name="zg%d" % i, tag="zg%d" % (i % 3), bufs=1, align_bytes=64)
+            nc.scalar.copy(out=zg[i][:].rearrange("p b r k -> p (b r k)").bitcast(F32).rearrange("p (b r h) -> p b r h", b=2, h=2), in_=bank[:].rearrange("p b h r -> p b r h"))
+
+        def Zq(i):
+            zq[i] = quant(zg[i][:].rearrange("p b r k -> p (b r k)"), 2 * P, "zq%d" % i)
+
+        def Hp(b, g):
             i, bb = b // 2, b % 2
             cc, ss = zq[i]
-            hb = work.tile([P, 2, P, 4], BF16, name="hb%d" % b, tag="hb", bufs=3, align_bytes=64)
-            for g in range(2):
-                bank = psum.tile([P, 4, P], F32, name="xs%d_%d" % (b, g), tag="x", bufs=XB)
-                for t in range(4):
-                    o = (4 * g + t) * P
-                    nc.tensor.matmul_mx(out=bank[:, t, :], lhsT=w1_c[:, o:o + P].bitcast(X4), lhsT_scale=w1_s[:, o:o + P],
-                                        rhs=cc[:, bb * P:bb * P + P].bitcast(X4), rhs_scale=ss[:, bb * P:bb * P + P], start=True, stop=True)
-                nc.scalar.activation(out=hb[:, g], in_=bank[:].rearrange("p t m -> p m t"), func=ACT.Relu)
-            hq[b] = quant(hb[:].rearrange("p g m t -> p (g m t)"), 2 * P, "hq%d" % b)
+            if g == 0:
+                hb[b] = work.tile([P, 2, P, 4], BF16, name="hb%d" % b, tag="hb%d" % (b % 3), bufs=1, align_bytes=64)
+            bank = banks["h", b, g] = psum.tile([P, 4, P], F32, name="xs%d_%d" % (b, g), tag="x%d" % g)
+            for t in range(4):
+                o = (4 * g + t) * P
+                nc.tensor.matmul_mx(out=bank[:, t, :], lhsT=w1_c[:, o:o + P].bitcast(X4), lhsT_scale=w1_s[:, o:o + P],
+                                    rhs=cc[:, bb * P:bb * P + P].bitcast(X4), rhs_scale=ss[:, bb * P:bb * P + P], start=True, stop=True)
 
-        def weights(a, g):
-            wide, inter = WM["%d%d" % (a, g)]
+        def Hr(b, g):
+            nc.scalar.activation(out=hb[b][:, g], in_=banks["h", b, g][:].rearrange("p t m -> p m t"), func=ACT.Relu)
+
+        def Hq(b):
+            hq[b] = quant(hb[b][:].rearrange("p g m t -> p (g m t)"), 2 * P, "hq%d" % b)
+
+        def Wd(a, g):
+            wide = WM["%d%d" % (a, g)][0]
             src = by[a, g][:].bitcast(F8)
             dst = wd[a, g][:].rearrange("p t n -> p (t n)")
-            col = (a * 2 + g) * 4
             if wide == "s":
                 nc.scalar.copy(out=dst, in_=src)
             elif wide == "v":
                 nc.vector.tensor_copy(out=dst, in_=src)
+            elif wide == "h":
+                nc.scalar.copy(out=dst[:, 0:1024], in_=src[:, 0:1024])
+                nc.vector.tensor_copy(out=dst[:, 1024:2048], in_=src[:, 1024:2048])
+
+        def Wi(a, g, j):
+            inter = WM["%d%d" % (a, g)][1]
+            col = (a * 2 + g) * 4
+            src = wd[a, g][:, :, P * j:P * j + P].rearrange("p t n -> p n t")
+            dst = wi[a, g][:, P * j:P * j + P, :]
+            cs = sc[:, col + j:col + j + 1]
+            if inter[j] == "g":
+                nc.gpsimd.tensor_scalar(dst, src, cs, 0.0, MULT, ADD)
+            elif inter[j] == "s":
+                nc.scalar.activation(out=dst, in_=src, func=ACT.Copy, scale=cs)
             else:
-                for k in range(16):
-                    sl = slice(k * P, k * P + P)
-                    cs = sc[:, col + k % 4:col + k % 4 + 1]
-                    if wide == "S":
-                        nc.scalar.activation(out=dst[:, sl], in_=src[:, sl], func=ACT.Copy, scale=cs)
-                    else:
-                        nc.vector.tensor_scalar(dst[:, sl], src[:, sl], cs, None, MULT)
-            if inter in ("G", "V", "S"):
-                src = wd[a, g][:].rearrange("p t n -> p n t")
-                dst = wi[a, g][:]
-                if inter == "G":
-                    nc.gpsimd.tensor_scalar(dst, src, 1.0, 0.0, MULT, ADD)
-                elif inter == "V":
-                    nc.vector.tensor_copy(out=dst, in_=src)
-                else:
-                    nc.scalar.copy(out=dst, in_=src)
-            else:
-                for j in range(4):
-                    src = wd[a, g][:, :, P * j:P * j + P].rearrange("p t n -> p n t")
-                    dst = wi[a, g][:, P * j:P * j + P, :]
-                    cs = sc[:, col + j:col + j + 1]
-                    if inter[j] == "g":
-                        nc.gpsimd.tensor_scalar(dst, src, cs, 0.0, MULT, ADD)
-                    elif inter[j] == "s":
-                        nc.scalar.activation(out=dst, in_=src, func=ACT.Copy, scale=cs)
-                    else:
-                        nc.vector.tensor_scalar(dst, src, cs, None, MULT)
+                nc.vector.tensor_scalar(dst, src, cs, None, MULT)
+
+        def Wq(a, g):
             nc.vector.quantize_mx(out=w2c[a, g][:].bitcast(X4), scales=w2s[a, g][:], in_=wi[a, g][:].rearrange("p n t -> p (n t)"))
 
         def product(a, b, tag, bufs):
@@ -191,111 +202,272 @@ def tile_e2crankonelocallylinearbeliefstep_d2p_kernel(tc, zbar, mean, var, u, w1
                                     rhs=w2c[a, g][:].bitcast(X4), rhs_scale=w2s[a, g][:], start=(g == 0), stop=(g == 1))
             return bank
 
-        def u_step():
-            for k in range(2):
-                bank = psum.tile([P, 4, P], BF16, name="xu%d" % k, tag="x", bufs=XB)
-                for b in range(4):
-                    nc.tensor.transpose(bank[:, b, :], u_t[:, 4 * k + b, :], ident_b[:])
-                nc.scalar.copy(out=ut[:, 4 * k:4 * k + 4, :], in_=bank[:])
+        def Ut(k):
+            bank = banks["u", k] = psum.tile([P, 4, P], BF16, name="xu%d" % k, tag="x%d" % k)
+            for b in range(4):
+                nc.tensor.transpose(bank[:, b, :], u_t[:, 4 * k + b, :], ident_b[:])
 
-        def base_step(b):
-            bank = psum.tile([P, Z], F32, name="xb%d" % b, tag="x", bufs=XB)
+        def Uc(k):
+            bank = banks["u", k]
+            nc.scalar.copy(out=ut[:, 4 * k:4 * k + 4, :], in_=bank[:])
+
+        def Qp(b):
+            bank = banks["q", b] = psum.tile([P, Z], F32, name="xb%d" % b, tag="q%d" % (b % QB))
             nc.tensor.matmul(bank[:], lhsT=ut[:, b, :], rhs=bm[:], start=True, stop=False)
-            nc.tensor.matmul(bank[:], lhsT=ident_b[:], rhs=mean_t[:, b, :], start=False, stop=True)
+            nc.tensor.matmul(bank[:], lhsT=ident_b[:], rhs=mean_t[:, b, :], start=False, stop=b not in EP)
+            if b in EP:
+                nc.tensor.matmul(bank[:], lhsT=ident_f[:], rhs=osb[b][:], start=False, stop=True)
+
+        def Qc(b):
+            bank = banks["q", b]
             nc.scalar.copy(out=base[:, b, :], in_=bank[:])
 
-        def r_step(b):
-            r = product(1, b, "a", AB)
-            if b in AG:
-                rs = work.tile([P, Z], F32, name="rs%d" % b, tag="rs", bufs=2)
-                nc.scalar.activation(out=rs[:], in_=r[:], func=ACT.Copy, scale=CROSS)
-                nc.gpsimd.tensor_tensor(rvt[:, b, :], rs[:], var_t[:, b, :], op=MULT)
-            else:
-                nc.vector.scalar_tensor_tensor(rvt[:, b, :], r[:], CROSS, var_t[:, b, :], MULT, MULT)
-            jd = work.tile([P, Z], F32, name="jd%d" % b, tag="jd", bufs=1)
-            nc.vector.scalar_tensor_tensor(jd[:], r[:], INV, mean_t[:, b, :], MULT, MULT, accum_out=d_col[b][:])
-            js = work.tile([P, Z], F32, name="js%d" % b, tag="js", bufs=1)
-            nc.vector.scalar_tensor_tensor(js[:], r[:], 1.0 / (Z * CROSS), rvt[:, b, :], MULT, MULT, accum_out=s_col[b][:])
+        def Op(b):
+            prods[2, b] = product(2, b, "o%d" % (b % OB), 1)
 
-        def v_step(b):
-            v = product(0, b, "a", AB)
-            sv = work.tile([P, Z], F32, name="sv%d" % b, tag="sv", bufs=3)
-            if b in DG:
-                tmp = work.tile([P, Z], F32, name="st%d" % b, tag="st", bufs=2)
-                nc.scalar.activation(out=tmp[:], in_=v[:], func=ACT.Copy, scale=s_col[b][:])
-                nc.gpsimd.tensor_tensor(sv[:], tmp[:], rvt[:, b, :], op=ADD)
-            else:
-                nc.vector.scalar_tensor_tensor(sv[:], v[:], s_col[b][:], rvt[:, b, :], MULT, ADD)
-            t3[b] = work.tile([P, Z], F32, name="t3_%d" % b, tag="t3", bufs=4)
-            nc.vector.scalar_tensor_tensor(t3[b][:], v[:], d_col[b][:], base[:, b, :], MULT, ADD)
-            t2 = work.tile([P, Z], F32, name="t2_%d" % b, tag="t2", bufs=3)
-            nc.vector.tensor_tensor(t2[:], v[:], sv[:], op=MULT)
-            vo = work.tile([P, Z], F32, name="vo_%d" % b, tag="vo", bufs=5)
-            if b in DV:
-                nc.vector.tensor_tensor(vo[:], t2[:], var_t[:, b, :], op=ADD)
-            else:
-                nc.gpsimd.tensor_tensor(vo[:], t2[:], var_t[:, b, :], op=ADD)
+        def Oc(b):
+            if b in EP:
+                osb[b] = work.tile([P, Z], F32, name="osb%d" % b, tag="osb%d" % (b % 3), bufs=1)
+                nc.scalar.copy(out=osb[b][:], in_=prods[2, b][:])
+
+        def Rp(b):
+            prods[1, b] = product(1, b, "a%d" % (b % AB), 1)
+
+        def Vp(b):
+            prods[0, b] = product(0, b, "a%d" % ((b + 8) % AB), 1)
+
+        def A(b):
+            nc.vector.scalar_tensor_tensor(rvt[:, b, :], prods[1, b][:], CROSS, var_t[:, b, :], MULT, MULT)
+
+        def C(b):
+            jd = work.tile([P, Z], F32, name="jd%d" % b, tag="jd", bufs=1)
+            nc.vector.scalar_tensor_tensor(jd[:], prods[1, b][:], INV, mean_t[:, b, :], MULT, MULT, accum_out=d_col[b][:])
+
+        def S(b):
+            js = work.tile([P, Z], F32, name="js%d" % b, tag="js", bufs=1)
+            nc.vector.scalar_tensor_tensor(js[:], prods[1, b][:], 1.0 / (Z * CROSS), rvt[:, b, :], MULT, MULT, accum_out=s_col[b][:])
+
+        def D1(b):
+            sv[b] = work.tile([P, Z], F32, name="sv%d" % b, tag="sv%d" % (b % 2), bufs=1)
+            nc.vector.scalar_tensor_tensor(sv[b][:], prods[0, b][:], s_col[b][:], rvt[:, b, :], MULT, ADD)
+
+        def D2(b):
+            tv[b] = work.tile([P, Z], F32, name="t2_%d" % b, tag="t2%d" % (b % 3), bufs=1)
+            nc.vector.tensor_tensor(tv[b][:], prods[0, b][:], sv[b][:], op=MULT)
+
+        def D3(b):
+            vo = work.tile([P, Z], F32, name="vo_%d" % b, tag="vo%d" % (b % 5), bufs=1)
+            eng = nc.vector if b in DV else nc.gpsimd
+            eng.tensor_tensor(vo[:], tv[b][:], var_t[:, b, :], op=ADD)
             nc.sync.dma_start(out=out1_v[:, b, :], in_=vo[:])
 
-        def o_step(b):
-            o = product(2, b, "o", OB)
-            mo = work.tile([P, Z], F32, name="mo_%d" % b, tag="mo", bufs=5)
-            if b in EG:
-                oc = work.tile([P, Z], F32, name="os%d" % b, tag="os", bufs=2)
-                nc.scalar.copy(out=oc[:], in_=o[:])
-                nc.gpsimd.tensor_tensor(mo[:], oc[:], t3[b][:], op=ADD)
-            else:
-                nc.vector.tensor_tensor(mo[:], o[:], t3[b][:], op=ADD)
-            nc.sync.dma_start(out=out0_v[:, b, :], in_=mo[:])
+        def E1(b):
+            t3[b] = work.tile([P, Z], F32, name="t3_%d" % b, tag="t3%d" % (b % 4), bufs=1)
+            nc.vector.scalar_tensor_tensor(t3[b][:], prods[0, b][:], d_col[b][:], base[:, b, :], MULT, ADD)
+            if b in EP:
+                nc.sync.dma_start(out=out0_v[:, b, :], in_=t3[b][:])
 
-        weights(1, 0)
-        pair(0)
-        weights(1, 1)
-        hidden(0)
-        pair(1)
-        hidden(1)
-        weights(0, 0)
-        r_step(0)
-        pair(2)
-        hidden(2)
-        weights(0, 1)
-        r_step(1)
-        pair(3)
-        hidden(3)
-        weights(2, 0)
-        u_step()
-        r_step(2)
-        base_step(0)
-        weights(2, 1)
-        r_step(3)
-        base_step(1)
-        v_step(0)
-        hidden(4)
-        r_step(4)
-        base_step(2)
-        v_step(1)
-        o_step(0)
-        hidden(5)
-        r_step(5)
-        base_step(3)
-        v_step(2)
-        o_step(1)
-        hidden(6)
-        r_step(6)
-        base_step(4)
-        v_step(3)
-        o_step(2)
-        hidden(7)
-        r_step(7)
-        base_step(5)
-        v_step(4)
-        o_step(3)
-        base_step(6)
-        v_step(5)
-        o_step(4)
-        base_step(7)
-        v_step(6)
-        o_step(5)
-        v_step(7)
-        o_step(6)
-        o_step(7)
+        def E2(b):
+            if b not in EP:
+                mo = work.tile([P, Z], F32, name="mo_%d" % b, tag="mo%d" % (b % 5), bufs=1)
+                nc.vector.tensor_tensor(mo[:], prods[2, b][:], t3[b][:], op=ADD)
+                nc.sync.dma_start(out=out0_v[:, b, :], in_=mo[:])
+        Pm(0)
+        Wd(1,0)
+        Pm(1)
+        Zp(0)
+        Wi(1,0,2)
+        Wd(1,1)
+        Zc(0)
+        Wi(1,1,3)
+        Wi(1,0,0)
+        Wi(1,0,3)
+        Zq(0)
+        Pm(2)
+        Wd(2,0)
+        Wi(1,1,1)
+        Wi(1,0,1)
+        Hp(0,0)
+        Wi(1,1,2)
+        Wi(1,1,0)
+        Wi(2,0,1)
+        Hp(0,1)
+        Hr(0,1)
+        Zp(1)
+        Hr(0,0)
+        Hp(1,0)
+        Zc(1)
+        Hp(1,1)
+        Wd(2,1)
+        Wq(1,0)
+        Wi(2,0,2)
+        Hq(0)
+        Wq(1,1)
+        Zq(1)
+        Hr(1,1)
+        Rp(0)
+        Wi(2,0,3)
+        C(0)
+        Hr(1,0)
+        Hq(1)
+        Wi(2,0,0)
+        A(0)
+        Zp(2)
+        Wi(2,1,0)
+        Wd(0,0)
+        Zc(2)
+        Wi(2,1,2)
+        Hp(2,1)
+        S(0)
+        Rp(1)
+        Wi(2,1,1)
+        Hp(2,0)
+        Hr(2,1)
+        Hr(2,0)
+        Wq(2,0)
+        Wi(0,0,2)
+        Wi(2,1,3)
+        Wi(0,0,1)
+        Hp(3,0)
+        Hq(2)
+        Wi(0,0,0)
+        Zq(2)
+        Zp(3)
+        Wd(0,1)
+        Rp(2)
+        Zc(3)
+        Hp(3,1)
+        Wi(0,0,3)
+        Hr(3,0)
+        Wq(2,1)
+        A(1)
+        Zq(3)
+        Hr(3,1)
+        Hp(4,0)
+        Op(1)
+        Wi(0,1,0)
+        A(2)
+        Hr(4,0)
+        Hq(3)
+        Oc(1)
+        Hp(4,1)
+        Hp(5,0)
+        Op(0)
+        S(2)
+        Hr(4,1)
+        Oc(0)
+        Hr(5,0)
+        Hp(5,1)
+        C(1)
+        Rp(3)
+        S(1)
+        Hq(4)
+        Hp(6,0)
+        Hr(5,1)
+        Hr(6,0)
+        Wq(0,0)
+        Hp(6,1)
+        C(2)
+        Rp(4)
+        Hr(6,1)
+        Hq(5)
+        C(3)
+        Ut(0)
+        Ut(1)
+        Rp(5)
+        Wi(0,1,3)
+        C(5)
+        Uc(0)
+        Uc(1)
+        A(5)
+        A(3)
+        A(4)
+        S(3)
+        C(4)
+        Hq(6)
+        Qp(0)
+        Wi(0,1,2)
+        Op(2)
+        Wi(0,1,1)
+        Op(3)
+        S(5)
+        Qc(0)
+        Hp(7,0)
+        Qp(1)
+        Rp(6)
+        Hp(7,1)
+        Wq(0,1)
+        S(4)
+        Oc(2)
+        Qc(1)
+        Hr(7,0)
+        Hr(7,1)
+        Oc(3)
+        C(6)
+        A(6)
+        Hq(7)
+        Vp(0)
+        Qp(2)
+        Qc(2)
+        D1(0)
+        Rp(7)
+        D2(0)
+        Op(4)
+        A(7)
+        S(6)
+        C(7)
+        Qp(3)
+        Oc(4)
+        Vp(1)
+        S(7)
+        D1(1)
+        Op(5)
+        Qc(3)
+        Oc(5)
+        Vp(2)
+        E1(0)
+        Qp(4)
+        Vp(3)
+        E1(2)
+        E1(1)
+        Op(6)
+        Qc(4)
+        Oc(6)
+        Qp(5)
+        Qc(5)
+        D3(0)
+        D2(1)
+        Op(7)
+        D1(3)
+        Vp(4)
+        Qp(6)
+        D2(3)
+        D1(2)
+        E1(3)
+        D3(1)
+        D3(3)
+        Qc(6)
+        Oc(7)
+        D2(2)
+        Vp(5)
+        D1(4)
+        D2(4)
+        E1(4)
+        D3(2)
+        Vp(7)
+        E1(5)
+        D1(5)
+        D3(4)
+        Qp(7)
+        Vp(6)
+        Qc(7)
+        D2(5)
+        D1(7)
+        D2(7)
+        D3(5)
+        D1(6)
+        E1(6)
+        D3(7)
+        D2(6)
+        D3(6)
+        E1(7)

@@ -74,10 +74,10 @@ def tile_e2crankonelocallylinearbeliefstep_d2p_kernel(tc, zbar, mean, var, u, w1
         out1_v = out_1.rearrange("(p b) n -> p b n", b=NT)
         w2_v = w2_bytes.rearrange("a (g p t) n -> a g p (t n)", g=2, t=4)
 
-        WM = {"10": ["h", "ssvs"], "11": ["v", "svsv"], "20": ["v", "svvv"], "21": ["h", "svvv"], "00": ["h", "vvsv"], "01": ["h", "vssv"]}
-        DV = [6]
+        WM = {"10":["v","ssvs"],"11":["v","vsvs"],"20":["v","vvsv"],"21":["v","vsvs"],"00":["v","ssss"],"01":["s","vsss"]}
+        DV = [0,1,2,3,4,5,6,7]
         AG = []
-        EP = [0, 1, 2, 3, 4, 5, 6, 7]
+        EP = [0,1,2,3,4,5,6,7]
         XB, AB, OB, QB = 2, 3, 2, 1
         nc.vector.memset(w1_sraw[:].bitcast(I32), 0)
         nc.gpsimd.dma_start(out=sc_all[:], in_=w2_scale.rearrange("a i j -> (a i j)").partition_broadcast(P))
@@ -152,7 +152,7 @@ def tile_e2crankonelocallylinearbeliefstep_d2p_kernel(tc, zbar, mean, var, u, w1
         def Hp(b, g):
             i, bb = b // 2, b % 2
             cc, ss = zq[i]
-            if g == 0:
+            if b not in hb:
                 hb[b] = work.tile([P, 2, P, 4], BF16, name="hb%d" % b, tag="hb%d" % (b % 3), bufs=1, align_bytes=64)
             bank = banks["h", b, g] = psum.tile([P, 4, P], F32, name="xs%d_%d" % (b, g), tag="x%d" % g)
             for t in range(4):
@@ -272,202 +272,203 @@ def tile_e2crankonelocallylinearbeliefstep_d2p_kernel(tc, zbar, mean, var, u, w1
                 mo = work.tile([P, Z], F32, name="mo_%d" % b, tag="mo%d" % (b % 5), bufs=1)
                 nc.vector.tensor_tensor(mo[:], prods[2, b][:], t3[b][:], op=ADD)
                 nc.sync.dma_start(out=out0_v[:, b, :], in_=mo[:])
-        Pm(0)
+
         Wd(1,0)
-        Pm(1)
+        Pm(0)
+        Wi(1,0,3)
         Zp(0)
         Wi(1,0,2)
-        Wd(1,1)
         Zc(0)
-        Wi(1,1,3)
-        Wi(1,0,0)
-        Wi(1,0,3)
-        Zq(0)
         Pm(2)
-        Wd(2,0)
-        Wi(1,1,1)
+        Wi(1,0,0)
+        Zq(0)
+        Pm(1)
         Wi(1,0,1)
-        Hp(0,0)
-        Wi(1,1,2)
-        Wi(1,1,0)
-        Wi(2,0,1)
         Hp(0,1)
+        Wd(1,1)
+        Hp(0,0)
         Hr(0,1)
-        Zp(1)
+        Wd(2,0)
         Hr(0,0)
+        Zp(1)
+        Wi(1,1,1)
         Hp(1,0)
+        Wi(1,1,2)
         Zc(1)
-        Hp(1,1)
-        Wd(2,1)
-        Wq(1,0)
-        Wi(2,0,2)
         Hq(0)
-        Wq(1,1)
-        Zq(1)
-        Hr(1,1)
-        Rp(0)
-        Wi(2,0,3)
-        C(0)
+        Wi(1,1,0)
         Hr(1,0)
-        Hq(1)
-        Wi(2,0,0)
-        A(0)
+        Hp(1,1)
+        Zq(1)
+        Wi(1,1,3)
+        Wi(2,0,3)
+        Wq(1,0)
         Zp(2)
-        Wi(2,1,0)
-        Wd(0,0)
-        Zc(2)
-        Wi(2,1,2)
+        Hr(1,1)
+        Wq(1,1)
+        Wi(2,0,2)
         Hp(2,1)
-        S(0)
-        Rp(1)
-        Wi(2,1,1)
-        Hp(2,0)
+        Wd(2,1)
+        Zc(2)
         Hr(2,1)
-        Hr(2,0)
-        Wq(2,0)
-        Wi(0,0,2)
-        Wi(2,1,3)
-        Wi(0,0,1)
-        Hp(3,0)
-        Hq(2)
-        Wi(0,0,0)
-        Zq(2)
+        Wi(2,0,0)
+        Hp(2,0)
+        Wi(2,1,1)
+        Wi(2,1,2)
+        Wd(0,0)
         Zp(3)
-        Wd(0,1)
-        Rp(2)
+        Hr(2,0)
+        Rp(0)
         Zc(3)
+        Wi(2,1,0)
+        Hp(3,0)
+        Wi(2,1,3)
+        Wi(2,0,1)
         Hp(3,1)
-        Wi(0,0,3)
+        Hq(2)
         Hr(3,0)
-        Wq(2,1)
-        A(1)
-        Zq(3)
+        Hq(1)
+        Zq(2)
+        Rp(2)
         Hr(3,1)
+        Wq(2,0)
+        Rp(1)
+        Wd(0,1)
+        A(0)
         Hp(4,0)
-        Op(1)
-        Wi(0,1,0)
-        A(2)
-        Hr(4,0)
-        Hq(3)
-        Oc(1)
-        Hp(4,1)
-        Hp(5,0)
+        Wq(2,1)
+        S(0)
         Op(0)
-        S(2)
+        Hp(4,1)
+        Hq(3)
+        Hr(4,0)
+        Op(1)
+        C(0)
         Hr(4,1)
-        Oc(0)
-        Hr(5,0)
+        A(1)
+        Hp(5,0)
+        Oc(1)
+        Zq(3)
         Hp(5,1)
-        C(1)
+        Oc(0)
+        A(2)
         Rp(3)
-        S(1)
+        Hr(5,0)
         Hq(4)
-        Hp(6,0)
+        S(1)
+        Op(2)
         Hr(5,1)
-        Hr(6,0)
-        Wq(0,0)
+        Hp(6,0)
+        C(1)
+        Wi(0,0,0)
         Hp(6,1)
+        Wi(0,1,0)
+        Hr(6,0)
+        Op(3)
         C(2)
+        Wi(0,1,3)
+        Hq(5)
+        Ut(0)
+        S(2)
         Rp(4)
         Hr(6,1)
-        Hq(5)
         C(3)
-        Ut(0)
+        Oc(2)
         Ut(1)
-        Rp(5)
-        Wi(0,1,3)
-        C(5)
         Uc(0)
+        Rp(5)
+        A(3)
+        Wi(0,0,2)
+        A(4)
+        Qp(0)
+        S(3)
+        Wi(0,0,1)
+        C(4)
+        Wi(0,0,3)
+        Hp(7,0)
+        Hq(6)
         Uc(1)
         A(5)
-        A(3)
-        A(4)
-        S(3)
-        C(4)
-        Hq(6)
-        Qp(0)
         Wi(0,1,2)
-        Op(2)
-        Wi(0,1,1)
-        Op(3)
-        S(5)
-        Qc(0)
-        Hp(7,0)
-        Qp(1)
-        Rp(6)
-        Hp(7,1)
-        Wq(0,1)
         S(4)
-        Oc(2)
-        Qc(1)
-        Hr(7,0)
-        Hr(7,1)
-        Oc(3)
-        C(6)
-        A(6)
-        Hq(7)
-        Vp(0)
-        Qp(2)
-        Qc(2)
-        D1(0)
-        Rp(7)
-        D2(0)
+        Hp(7,1)
+        Qc(0)
         Op(4)
-        A(7)
-        S(6)
+        Wq(0,0)
+        Rp(6)
+        Wi(0,1,1)
+        C(5)
+        Hr(7,0)
+        Qp(1)
+        S(5)
+        Hr(7,1)
+        Wq(0,1)
+        Oc(3)
+        Hq(7)
+        Qc(1)
+        C(6)
+        Rp(7)
+        A(6)
+        Vp(0)
         C(7)
-        Qp(3)
-        Oc(4)
+        Qp(2)
+        S(6)
+        D1(0)
+        Qc(2)
         Vp(1)
-        S(7)
-        D1(1)
+        A(7)
+        Oc(4)
         Op(5)
+        D2(0)
+        S(7)
+        Qp(3)
+        D1(1)
         Qc(3)
-        Oc(5)
+        D3(0)
         Vp(2)
-        E1(0)
-        Qp(4)
-        Vp(3)
-        E1(2)
+        Oc(5)
         E1(1)
-        Op(6)
+        D2(1)
+        E1(0)
+        Vp(4)
+        D3(1)
+        Vp(3)
+        D1(2)
+        Qp(4)
+        E1(2)
+        D2(2)
+        D1(3)
         Qc(4)
+        Vp(5)
+        E1(3)
+        Op(6)
+        D1(4)
         Oc(6)
         Qp(5)
-        Qc(5)
-        D3(0)
-        D2(1)
-        Op(7)
-        D1(3)
-        Vp(4)
-        Qp(6)
         D2(3)
-        D1(2)
-        E1(3)
-        D3(1)
-        D3(3)
-        Qc(6)
-        Oc(7)
-        D2(2)
-        Vp(5)
-        D1(4)
-        D2(4)
         E1(4)
+        Qc(5)
         D3(2)
-        Vp(7)
-        E1(5)
-        D1(5)
-        D3(4)
-        Qp(7)
         Vp(6)
-        Qc(7)
+        D1(5)
+        D2(4)
+        D3(3)
+        Vp(7)
         D2(5)
-        D1(7)
-        D2(7)
-        D3(5)
+        Qp(6)
+        D3(4)
         D1(6)
+        D1(7)
+        Qc(6)
+        Op(7)
+        D2(6)
+        Oc(7)
+        D3(5)
+        Qp(7)
+        D3(6)
+        D2(7)
+        Qc(7)
         E1(6)
         D3(7)
-        D2(6)
-        D3(6)
+        E1(5)
         E1(7)

from contextlib import ExitStack

import concourse.mybir as mybir
from concourse.masks import make_identity

B, Z, F, U, T = 1024, 512, 1024, 128, 3
P = 128
NT = B // P
FLOPS = 2 * B * Z * F + 2 * T * B * F * Z + 2 * B * U * Z

F32 = mybir.dt.float32
BF16 = mybir.dt.bfloat16
U32 = mybir.dt.uint32
I32 = mybir.dt.int32
U8 = mybir.dt.uint8
F8 = mybir.dt.float8_e4m3fn
X4 = mybir.dt.float8_e4m3fn_x4
ADD = mybir.AluOpType.add
MULT = mybir.AluOpType.mult
ACT = mybir.ActivationFunctionType

INV = 1.0 / Z ** 0.5
CROSS = 2.0 * INV


def tile_e2crankonelocallylinearbeliefstep_d2p_kernel(tc, zbar, mean, var, u, w1_words, w1_scales, w2_bytes, w2_scale, bmat, out_0, out_1):
    nc = tc.nc
    with ExitStack() as ctx:
        keep = ctx.enter_context(tc.tile_pool(name="keep", bufs=1))
        work = ctx.enter_context(tc.tile_pool(name="work", bufs=3))
        psum = ctx.enter_context(tc.psum_pool(name="psum", bufs=1))
        ctx.enter_context(tc.manual_schedule())

        def kt(name, shape, dtype):
            return keep.tile(shape, dtype, name=name, align_bytes=64)

        ident_f = kt("ident_f", [P, P], F32)
        ident_b = kt("ident_b", [P, P], BF16)
        zb = kt("zb", [P, NT, Z], BF16)
        w1_raw = kt("w1_raw", [P, F], U32)
        w1_sraw = kt("w1_sraw", [P, F], U8)
        w1_c = kt("w1_c", [P, F], U32)
        w1_s = kt("w1_s", [P, F], U8)
        sc_all = kt("sc_all", [P, 96], F32)
        sc = kt("sc", [P, 24], F32)
        by = {}
        wd = {}
        wi = {}
        w2c = {}
        w2s = {}
        for a in range(3):
            for g in range(2):
                by[a, g] = kt("by%d%d" % (a, g), [P, 4 * Z], U8)
                wd[a, g] = kt("wd%d%d" % (a, g), [P, 4, Z], BF16)
                wi[a, g] = kt("wi%d%d" % (a, g), [P, Z, 4], BF16)
                w2c[a, g] = kt("w2c%d%d" % (a, g), [P, Z], U32)
                w2s[a, g] = kt("w2s%d%d" % (a, g), [P, Z], U8)
        mean_t = kt("mean_t", [P, NT, Z], BF16)
        var_t = kt("var_t", [P, NT, Z], BF16)
        u_t = kt("u_t", [P, NT, U], BF16)
        ut = kt("ut", [P, NT, P], BF16)
        bm = kt("bm", [P, Z], BF16)
        base = kt("base", [P, NT, Z], F32)
        rvt = kt("rvt", [P, NT, Z], F32)
        junk = kt("junk", [P, Z], F32)
        d_col = [kt("d%d" % b, [P, 1], F32) for b in range(NT)]
        s_col = [kt("s%d" % b, [P, 1], F32) for b in range(NT)]

        zbar_v = zbar.rearrange("(p b) k -> p b k", b=NT)
        mean_v = mean.rearrange("(p b) k -> p b k", b=NT)
        var_v = var.rearrange("(p b) k -> p b k", b=NT)
        u_v = u.rearrange("(p b) k -> p b k", b=NT)
        out0_v = out_0.rearrange("(p b) n -> p b n", b=NT)
        out1_v = out_1.rearrange("(p b) n -> p b n", b=NT)
        w2_v = w2_bytes.rearrange("a (g p t) n -> a g p (t n)", g=2, t=4)

        WM = {"10":["v","ssvs"],"11":["v","vsvs"],"20":["v","vvsv"],"21":["v","vsvs"],"00":["v","ssss"],"01":["s","vsss"]}
        DV = [0,1,2,3,4,5,6,7]
        AG = []
        EP = [0,1,2,3,4,5,6,7]
        XB, AB, OB, QB = 2, 3, 2, 1
        nc.vector.memset(w1_sraw[:].bitcast(I32), 0)
        nc.gpsimd.dma_start(out=sc_all[:], in_=w2_scale.rearrange("a i j -> (a i j)").partition_broadcast(P))
        nc.sync.dma_start(out=by[1, 0][:], in_=w2_v[1, 0])
        for q in range(4):
            nc.sync.dma_start(out=w1_sraw[32 * q:32 * q + 4, :].bitcast(I32), in_=w1_scales[0, 4 * q:4 * q + 4, :].bitcast(I32))
        nc.sync.dma_start(out=zb[:, 0:2, :], in_=zbar_v[:, 0:2, :])
        nc.sync.dma_start(out=w1_raw[:].bitcast(I32), in_=w1_words[0].rearrange("p n t -> p (n t)").bitcast(I32))
        nc.sync.dma_start(out=by[1, 1][:], in_=w2_v[1, 1])
        nc.sync.dma_start(out=zb[:, 2:4, :], in_=zbar_v[:, 2:4, :])
        nc.sync.dma_start(out=by[2, 0][:], in_=w2_v[2, 0])
        nc.sync.dma_start(out=by[2, 1][:], in_=w2_v[2, 1])
        nc.sync.dma_start(out=zb[:, 4:6, :], in_=zbar_v[:, 4:6, :])
        nc.sync.dma_start(out=zb[:, 6:8, :], in_=zbar_v[:, 6:8, :])
        nc.sync.dma_start(out=var_t[:, 0:4, :], in_=var_v[:, 0:4, :])
        nc.sync.dma_start(out=mean_t[:, 0:4, :], in_=mean_v[:, 0:4, :])
        nc.sync.dma_start(out=u_t[:], in_=u_v)
        nc.sync.dma_start(out=bm[:], in_=bmat)
        nc.sync.dma_start(out=by[0, 0][:], in_=w2_v[0, 0])
        nc.sync.dma_start(out=by[0, 1][:], in_=w2_v[0, 1])
        nc.sync.dma_start(out=var_t[:, 4:8, :], in_=var_v[:, 4:8, :])
        nc.sync.dma_start(out=mean_t[:, 4:8, :], in_=mean_v[:, 4:8, :])

        make_identity(nc, ident_f[:])
        sc_view = sc_all[:].rearrange("p (a g q j) -> p q a g j", a=3, g=2, q=4, j=4)
        sc_out = sc[:].rearrange("p (a g j) -> p a g j", a=3, g=2, j=4)
        for q in range(4):
            nc.scalar.copy(out=sc_out[32 * q:32 * q + 32], in_=sc_view[32 * q:32 * q + 32, q])
        nc.scalar.copy(out=ident_b[:], in_=ident_f[:])
        def Pm(k):
            if k == 0:
                nc.vector.tensor_copy(out=w1_s[:].rearrange("p (g t m) -> p g t m", g=2, t=4), in_=w1_sraw[:].rearrange("p (g m t) -> p g t m", g=2, t=4))
            else:
                g = k - 1
                nc.vector.tensor_copy(out=w1_c[:, 512 * g:512 * g + 512].bitcast(I32).rearrange("p (t m) -> p t m", t=4), in_=w1_raw[:, 512 * g:512 * g + 512].bitcast(I32).rearrange("p (m t) -> p t m", t=4))

        banks = {}

        zwords = zb[:].rearrange("p b k -> p (b k)").bitcast(F32)
        zq = {}
        hq = {}
        t3 = {}

        def quant(x, width, name):
            cc = keep.tile([P, width], U32, name=name + "c", align_bytes=64)
            ss = keep.tile([P, width], U8, name=name + "s", align_bytes=64)
            nc.vector.quantize_mx(out=cc[:].bitcast(X4), scales=ss[:], in_=x)
            return cc, ss

        zg = {}
        hb = {}
        prods = {}
        osb = {}
        sv = {}
        tv = {}

        def Zp(i):
            bank = banks["z", i] = psum.tile([P, 2, 2, P], F32, name="xz%d" % i, tag="x%d" % (i % 2))
            for bb in range(2):
                o = (2 * i + bb) * 256
                for h in range(2):
                    nc.tensor.transpose(bank[:, bb, h, :], zwords[:, o + h:o + 256:2], ident_f[:])

        def Zc(i):
            bank = banks["z", i]
            zg[i] = work.tile([P, 2, P, 4], BF16, name="zg%d" % i, tag="zg%d" % (i % 3), bufs=1, align_bytes=64)
            nc.scalar.copy(out=zg[i][:].rearrange("p b r k -> p (b r k)").bitcast(F32).rearrange("p (b r h) -> p b r h", b=2, h=2), in_=bank[:].rearrange("p b h r -> p b r h"))

        def Zq(i):
            zq[i] = quant(zg[i][:].rearrange("p b r k -> p (b r k)"), 2 * P, "zq%d" % i)

        def Hp(b, g):
            i, bb = b // 2, b % 2
            cc, ss = zq[i]
            if b not in hb:
                hb[b] = work.tile([P, 2, P, 4], BF16, name="hb%d" % b, tag="hb%d" % (b % 3), bufs=1, align_bytes=64)
            bank = banks["h", b, g] = psum.tile([P, 4, P], F32, name="xs%d_%d" % (b, g), tag="x%d" % g)
            for t in range(4):
                o = (4 * g + t) * P
                nc.tensor.matmul_mx(out=bank[:, t, :], lhsT=w1_c[:, o:o + P].bitcast(X4), lhsT_scale=w1_s[:, o:o + P],
                                    rhs=cc[:, bb * P:bb * P + P].bitcast(X4), rhs_scale=ss[:, bb * P:bb * P + P], start=True, stop=True)

        def Hr(b, g):
            nc.scalar.activation(out=hb[b][:, g], in_=banks["h", b, g][:].rearrange("p t m -> p m t"), func=ACT.Relu)

        def Hq(b):
            hq[b] = quant(hb[b][:].rearrange("p g m t -> p (g m t)"), 2 * P, "hq%d" % b)

        def Wd(a, g):
            wide = WM["%d%d" % (a, g)][0]
            src = by[a, g][:].bitcast(F8)
            dst = wd[a, g][:].rearrange("p t n -> p (t n)")
            if wide == "s":
                nc.scalar.copy(out=dst, in_=src)
            elif wide == "v":
                nc.vector.tensor_copy(out=dst, in_=src)
            elif wide == "h":
                nc.scalar.copy(out=dst[:, 0:1024], in_=src[:, 0:1024])
                nc.vector.tensor_copy(out=dst[:, 1024:2048], in_=src[:, 1024:2048])

        def Wi(a, g, j):
            inter = WM["%d%d" % (a, g)][1]
            col = (a * 2 + g) * 4
            src = wd[a, g][:, :, P * j:P * j + P].rearrange("p t n -> p n t")
            dst = wi[a, g][:, P * j:P * j + P, :]
            cs = sc[:, col + j:col + j + 1]
            if inter[j] == "g":
                nc.gpsimd.tensor_scalar(dst, src, cs, 0.0, MULT, ADD)
            elif inter[j] == "s":
                nc.scalar.activation(out=dst, in_=src, func=ACT.Copy, scale=cs)
            else:
                nc.vector.tensor_scalar(dst, src, cs, None, MULT)

        def Wq(a, g):
            nc.vector.quantize_mx(out=w2c[a, g][:].bitcast(X4), scales=w2s[a, g][:], in_=wi[a, g][:].rearrange("p n t -> p (n t)"))

        def product(a, b, tag, bufs):
            bank = psum.tile([P, Z], F32, name="ps%d_%d" % (a, b), tag=tag, bufs=bufs)
            cc, ss = hq[b]
            for g in range(2):
                nc.tensor.matmul_mx(out=bank[:], lhsT=cc[:, g * P:g * P + P].bitcast(X4), lhsT_scale=ss[:, g * P:g * P + P],
                                    rhs=w2c[a, g][:].bitcast(X4), rhs_scale=w2s[a, g][:], start=(g == 0), stop=(g == 1))
            return bank

        def Ut(k):
            bank = banks["u", k] = psum.tile([P, 4, P], BF16, name="xu%d" % k, tag="x%d" % k)
            for b in range(4):
                nc.tensor.transpose(bank[:, b, :], u_t[:, 4 * k + b, :], ident_b[:])

        def Uc(k):
            bank = banks["u", k]
            nc.scalar.copy(out=ut[:, 4 * k:4 * k + 4, :], in_=bank[:])

        def Qp(b):
            bank = banks["q", b] = psum.tile([P, Z], F32, name="xb%d" % b, tag="q%d" % (b % QB))
            nc.tensor.matmul(bank[:], lhsT=ut[:, b, :], rhs=bm[:], start=True, stop=False)
            nc.tensor.matmul(bank[:], lhsT=ident_b[:], rhs=mean_t[:, b, :], start=False, stop=b not in EP)
            if b in EP:
                nc.tensor.matmul(bank[:], lhsT=ident_f[:], rhs=osb[b][:], start=False, stop=True)

        def Qc(b):
            bank = banks["q", b]
            nc.scalar.copy(out=base[:, b, :], in_=bank[:])

        def Op(b):
            prods[2, b] = product(2, b, "o%d" % (b % OB), 1)

        def Oc(b):
            if b in EP:
                osb[b] = work.tile([P, Z], F32, name="osb%d" % b, tag="osb%d" % (b % 3), bufs=1)
                nc.scalar.copy(out=osb[b][:], in_=prods[2, b][:])

        def Rp(b):
            prods[1, b] = product(1, b, "a%d" % (b % AB), 1)

        def Vp(b):
            prods[0, b] = product(0, b, "a%d" % ((b + 8) % AB), 1)

        def A(b):
            nc.vector.scalar_tensor_tensor(rvt[:, b, :], prods[1, b][:], CROSS, var_t[:, b, :], MULT, MULT)

        def C(b):
            jd = work.tile([P, Z], F32, name="jd%d" % b, tag="jd", bufs=1)
            nc.vector.scalar_tensor_tensor(jd[:], prods[1, b][:], INV, mean_t[:, b, :], MULT, MULT, accum_out=d_col[b][:])

        def S(b):
            js = work.tile([P, Z], F32, name="js%d" % b, tag="js", bufs=1)
            nc.vector.scalar_tensor_tensor(js[:], prods[1, b][:], 1.0 / (Z * CROSS), rvt[:, b, :], MULT, MULT, accum_out=s_col[b][:])

        def D1(b):
            sv[b] = work.tile([P, Z], F32, name="sv%d" % b, tag="sv%d" % (b % 2), bufs=1)
            nc.vector.scalar_tensor_tensor(sv[b][:], prods[0, b][:], s_col[b][:], rvt[:, b, :], MULT, ADD)

        def D2(b):
            tv[b] = work.tile([P, Z], F32, name="t2_%d" % b, tag="t2%d" % (b % 3), bufs=1)
            nc.vector.tensor_tensor(tv[b][:], prods[0, b][:], sv[b][:], op=MULT)

        def D3(b):
            vo = work.tile([P, Z], F32, name="vo_%d" % b, tag="vo%d" % (b % 5), bufs=1)
            eng = nc.vector if b in DV else nc.gpsimd
            eng.tensor_tensor(vo[:], tv[b][:], var_t[:, b, :], op=ADD)
            nc.sync.dma_start(out=out1_v[:, b, :], in_=vo[:])

        def E1(b):
            t3[b] = work.tile([P, Z], F32, name="t3_%d" % b, tag="t3%d" % (b % 4), bufs=1)
            nc.vector.scalar_tensor_tensor(t3[b][:], prods[0, b][:], d_col[b][:], base[:, b, :], MULT, ADD)
            if b in EP:
                nc.sync.dma_start(out=out0_v[:, b, :], in_=t3[b][:])

        def E2(b):
            if b not in EP:
                mo = work.tile([P, Z], F32, name="mo_%d" % b, tag="mo%d" % (b % 5), bufs=1)
                nc.vector.tensor_tensor(mo[:], prods[2, b][:], t3[b][:], op=ADD)
                nc.sync.dma_start(out=out0_v[:, b, :], in_=mo[:])

        Wd(1,0)
        Pm(0)
        Wi(1,0,3)
        Zp(0)
        Wi(1,0,2)
        Zc(0)
        Pm(2)
        Wi(1,0,0)
        Zq(0)
        Pm(1)
        Wi(1,0,1)
        Hp(0,1)
        Wd(1,1)
        Hp(0,0)
        Hr(0,1)
        Wd(2,0)
        Hr(0,0)
        Zp(1)
        Wi(1,1,1)
        Hp(1,0)
        Wi(1,1,2)
        Zc(1)
        Hq(0)
        Wi(1,1,0)
        Hr(1,0)
        Hp(1,1)
        Zq(1)
        Wi(1,1,3)
        Wi(2,0,3)
        Wq(1,0)
        Zp(2)
        Hr(1,1)
        Wq(1,1)
        Wi(2,0,2)
        Hp(2,1)
        Wd(2,1)
        Zc(2)
        Hr(2,1)
        Wi(2,0,0)
        Hp(2,0)
        Wi(2,1,1)
        Wi(2,1,2)
        Wd(0,0)
        Zp(3)
        Hr(2,0)
        Rp(0)
        Zc(3)
        Wi(2,1,0)
        Hp(3,0)
        Wi(2,1,3)
        Wi(2,0,1)
        Hp(3,1)
        Hq(2)
        Hr(3,0)
        Hq(1)
        Zq(2)
        Rp(2)
        Hr(3,1)
        Wq(2,0)
        Rp(1)
        Wd(0,1)
        A(0)
        Hp(4,0)
        Wq(2,1)
        S(0)
        Op(0)
        Hp(4,1)
        Hq(3)
        Hr(4,0)
        Op(1)
        C(0)
        Hr(4,1)
        A(1)
        Hp(5,0)
        Oc(1)
        Zq(3)
        Hp(5,1)
        Oc(0)
        A(2)
        Rp(3)
        Hr(5,0)
        Hq(4)
        S(1)
        Op(2)
        Hr(5,1)
        Hp(6,0)
        C(1)
        Wi(0,0,0)
        Hp(6,1)
        Wi(0,1,0)
        Hr(6,0)
        Op(3)
        C(2)
        Wi(0,1,3)
        Hq(5)
        Ut(0)
        S(2)
        Rp(4)
        Hr(6,1)
        C(3)
        Oc(2)
        Ut(1)
        Uc(0)
        Rp(5)
        A(3)
        Wi(0,0,2)
        A(4)
        Qp(0)
        S(3)
        Wi(0,0,1)
        C(4)
        Wi(0,0,3)
        Hp(7,0)
        Hq(6)
        Uc(1)
        A(5)
        Wi(0,1,2)
        S(4)
        Hp(7,1)
        Qc(0)
        Op(4)
        Wq(0,0)
        Rp(6)
        Wi(0,1,1)
        C(5)
        Hr(7,0)
        Qp(1)
        S(5)
        Hr(7,1)
        Wq(0,1)
        Oc(3)
        Hq(7)
        Qc(1)
        C(6)
        Rp(7)
        A(6)
        Vp(0)
        C(7)
        Qp(2)
        S(6)
        D1(0)
        Qc(2)
        Vp(1)
        A(7)
        Oc(4)
        Op(5)
        D2(0)
        S(7)
        Qp(3)
        D1(1)
        Qc(3)
        D3(0)
        Vp(2)
        Oc(5)
        E1(1)
        D2(1)
        E1(0)
        Vp(4)
        D3(1)
        Vp(3)
        D1(2)
        Qp(4)
        E1(2)
        D2(2)
        D1(3)
        Qc(4)
        Vp(5)
        E1(3)
        Op(6)
        D1(4)
        Oc(6)
        Qp(5)
        D2(3)
        E1(4)
        Qc(5)
        D3(2)
        Vp(6)
        D1(5)
        D2(4)
        D3(3)
        Vp(7)
        D2(5)
        Qp(6)
        D3(4)
        D1(6)
        D1(7)
        Qc(6)
        Op(7)
        D2(6)
        Oc(7)
        D3(5)
        Qp(7)
        D3(6)
        D2(7)
        Qc(7)
        E1(6)
        D3(7)
        E1(5)
        E1(7)
